import numpy as np
import ml_dtypes


def mxq(x, axis, fmt="e4m3"):
    dtype, down = {"e4m3": (ml_dtypes.float8_e4m3fn, 7), "e5m2": (ml_dtypes.float8_e5m2, 14)}[fmt]
    v = np.moveaxis(np.asarray(x, np.float32).astype(ml_dtypes.bfloat16).astype(np.float64), axis, -1)
    blocks = v.reshape(v.shape[:-1] + (-1, 32))
    amax = np.abs(blocks).max(-1, keepdims=True)
    byte = np.maximum(np.where(amax > 0, np.frexp(amax)[1] - 1 + 127, 0) - down, 1)
    scale = np.exp2(byte - 127.0)
    codes = (blocks / scale).astype(np.float32).astype(dtype).astype(np.float64)
    return np.moveaxis((codes * scale).reshape(v.shape), -1, axis)


WIDE = False


def mx_kscale(k):
    if not WIDE:
        return np.ones(k)
    levels = np.array([10, -10, 5, -5, 0])
    if k % 512:
        return np.exp2(np.random.permutation(np.resize(levels, k // 32))).repeat(32)
    a = np.empty((k // 512, 16))
    for p in range(k // 512):
        a[p, :8] = np.random.permutation(np.resize(levels, 8))
        for g in range(8):
            far = levels[np.abs(levels - a[p, g]) >= 10]
            a[p, g + 8] = far[np.random.randint(len(far))]
    return np.exp2(a.ravel()).repeat(32)


def f64(x):
    return np.asarray(x).astype(np.float64)


def striped(idx):
    return np.tile(idx.reshape(-1, 16).T, (8, 1)).astype(np.uint16)


def unstriped(offs):
    return offs[:16].T.reshape(-1).astype(np.int64)


def striped8(idx):
    return np.concatenate([x.reshape(-1, 16).T for x in idx]).astype(np.uint16)


def runs(offs, k):
    lists = np.stack([offs[16 * r : 16 * r + 16].T.reshape(-1) for r in range(8)]).astype(np.int64)
    return lists[np.arange(k) % 512 // 64]


def pack_weight(w):
    k, n = w.shape
    w = f64(np.asarray(w, np.float32).astype(ml_dtypes.bfloat16)).reshape(k // 32, 32, n)
    amax = np.abs(w).max(1)
    byte = np.clip(np.where(amax > 0, np.frexp(amax)[1] - 1 + 127 - 7, 1), 1, 254)
    scaled = (w * np.exp2(127.0 - byte)[:, None, :]).reshape(k, n).astype(np.float32)
    words = np.ascontiguousarray(scaled.reshape(k // 512, 128, 4, n).transpose(0, 1, 3, 2)).astype(ml_dtypes.float8_e4m3fn).view(np.uint8)
    return words, np.ascontiguousarray(byte.astype(np.uint8).reshape(k // 512, 16, n))


def unpack_weight(words, scales):
    g, p, n, _ = words.shape
    vals = np.ascontiguousarray(words).view(ml_dtypes.float8_e4m3fn).astype(np.float64) * np.repeat(np.exp2(scales.astype(np.float64) - 127.0), 8, axis=1)[..., None]
    return vals.transpose(0, 1, 3, 2).reshape(g * 512, n)


E2M1 = np.array([0.0, 0.5, 1.0, 1.5, 2.0, 3.0, 4.0, 6.0, -0.0, -0.5, -1.0, -1.5, -2.0, -3.0, -4.0, -6.0])


def pack_fp4(w):
    k, n = w.shape
    w = f64(np.asarray(w, np.float32).astype(ml_dtypes.bfloat16)).reshape(k // 32, 32, n)
    amax = np.abs(w).max(1)
    mant, ex = np.frexp(amax / 6.0)
    byte = np.clip(np.where(amax > 0, np.where(mant > 0.5, ex, ex - 1) + 127, 1), 1, 254)
    scaled = (w * np.exp2(127.0 - byte)[:, None, :]).reshape(k, n).astype(np.float32)
    c = np.ascontiguousarray(scaled.reshape(k // 512, 128, 4, n).transpose(0, 1, 3, 2)).astype(ml_dtypes.float4_e2m1fn).view(np.uint8) & 0xF
    words = (c[..., 0::2] | (c[..., 1::2] << 4)).reshape(k // 512, 128, 2 * n)
    return np.ascontiguousarray(words), np.ascontiguousarray(byte.astype(np.uint8).reshape(k // 512, 16, n))


def unpack_fp4(words, scales):
    g, _, n = scales.shape
    words = np.ascontiguousarray(words).reshape(g, 128, n, 2)
    nib = np.empty((g, 128, n, 4), np.uint8)
    nib[..., 0::2] = words & 0xF
    nib[..., 1::2] = words >> 4
    vals = E2M1[nib] * np.repeat(np.exp2(scales.astype(np.float64) - 127.0), 8, axis=1)[..., None]
    return vals.transpose(0, 1, 3, 2).reshape(g * 512, n)


def planes(y):
    n, m = y.shape
    v = y.astype(np.float32).astype(ml_dtypes.bfloat16).astype(np.float64).reshape(n // 32, 32, m)
    top = np.abs(v).max(1)
    byte = np.clip(np.where(top > 0, np.frexp(top)[1] - 1 + 127 - 7, 1), 1, 254)
    codes = (v * np.exp2(127.0 - byte)[:, None, :]).reshape(n, m).astype(np.float32).astype(ml_dtypes.float8_e4m3fn).view(np.uint8)
    words = codes.reshape(n // 512, 128, 4, m).transpose(0, 1, 3, 2)
    return np.ascontiguousarray(words), np.ascontiguousarray(byte.astype(np.uint8).reshape(n // 512, 16, m))


K, T, S, N, G, H, U = 512, 2048, 512, 512, 2048, 512, 1024


def setup_inputs():
    n = np.random.standard_normal
    s = mx_kscale(K)[:, None]
    u = mx_kscale(S)
    packed_xT = pack_weight(n((K, T)) * s)
    packed_dT = pack_weight(n((K, G)) / s)
    packed_w1 = pack_fp4(n((H, N)) / np.sqrt(H) / u[:, None])
    return {
        "x_words": packed_xT[0],
        "x_scales": packed_xT[1],
        "d_words": packed_dT[0],
        "d_scales": packed_dT[1],
        "gn": (np.random.uniform(0.5, 1.5, (H, 1)) * u[:, None]).astype(np.float32),
        "w1_words": packed_w1[0],
        "w1_scales": packed_w1[1],
        "mem": n((N, U)).astype(np.float32),
        "offs": striped(np.random.permutation(T)[:S]),
        "k1": striped8(np.random.randint(0, G, (8, H))),
        "n1": striped8(np.stack([np.random.permutation(S) for _ in range(8)])),
        "n2": striped8(np.stack([np.random.permutation(S) for _ in range(8)])),
        "n3": striped8(np.stack([np.random.permutation(S) for _ in range(8)])),
        "n4": striped(np.random.permutation(U)[:S]),
    }


def reference(x_words, x_scales, d_words, d_scales, gn, w1_words, w1_scales, mem, offs, k1, n1, n2, n3, n4):
    d_k1 = unpack_weight(d_words, d_scales)[np.arange(K)[:, None], runs(k1, K)]
    xq = unpack_weight(x_words, x_scales)[:, unstriped(offs)]
    h = 0.0625 * (d_k1.T @ xq)
    z = f64(gn) * (h + h[np.arange(H)[:, None], runs(n1, H)] - (np.maximum(h[np.arange(H)[:, None], runs(n2, H)], h[np.arange(H)[:, None], runs(n3, H)])))
    h2 = unpack_fp4(w1_words, w1_scales).T @ mxq(z, 0, "e4m3")
    out = f64(mem).copy()
    out[:, unstriped(n4)] = h2
    return (out,) + planes(out)

@@ -1,0 +1,219 @@
+from contextlib import ExitStack
+
+import concourse.mybir as mybir
+
+K, T, S, N, G, H, U = 512, 2048, 512, 512, 2048, 512, 1024
+FLOPS = 2 * K * H * S + 2 * H * N * S
+
+F32 = mybir.dt.float32
+BF16 = mybir.dt.bfloat16
+I32 = mybir.dt.int32
+U32 = mybir.dt.uint32
+U16 = mybir.dt.uint16
+U8 = mybir.dt.uint8
+FP8X4 = mybir.dt.float8_e4m3fn_x4
+FP4X4 = mybir.dt.float4_e2m1fn_x4
+ALU = mybir.AluOpType
+COPY = mybir.ActivationFunctionType.Copy
+
+P = 128
+PACK = 4
+CHUNK = 256
+CHUNKS = S // CHUNK
+LANES = 16
+
+
+def tile_picked_pqlaytrimpage_none_po_kernel(
+    tc, x_words, x_scales, d_words, d_scales, gn, w1_words, w1_scales, mem,
+    offs, k1, n1, n2, n3, n4, out_0, out_1, out_2,
+):
+    nc = tc.nc
+    with ExitStack() as ctx:
+        lists = ctx.enter_context(tc.tile_pool(name="lists", bufs=1))
+        keep = ctx.enter_context(tc.tile_pool(name="keep", bufs=1))
+        shared = ctx.enter_context(tc.tile_pool(name="shared", bufs=1))
+        psum = ctx.enter_context(tc.psum_pool(name="psum", bufs=1))
+
+        def load_list(src, name):
+            tile = lists.tile([P, S // LANES], U16, name=name)
+            nc.sync.dma_start(tile[:], src)
+            return tile
+
+        def entries(tile, c):
+            return tile[:, c * CHUNK // LANES : (c + 1) * CHUNK // LANES]
+
+        def sb(shape, dtype, name):
+            return keep.tile(shape, dtype, name=name, align_bytes=64)
+
+        ds_table = sb([P, G], U8, "ds_table")
+        xs_table = shared.tile([P, T], U8, name="xs_table", offset=15360)
+        nc.gpsimd.memset(xs_table[:].bitcast(I32), 0)
+
+        k1_t = load_list(k1, "k1_t")
+        nc.sync.dma_start(ds_table[:].bitcast(I32), d_scales[0].bitcast(I32).unsqueeze(1).to_broadcast([16, 8, G // 4]))
+        offs_t = load_list(offs, "offs_t")
+        n2_t = load_list(n2, "n2_t")
+        dw_table = shared.tile([P, G], U32, name="dw_table", offset=20480)
+        nc.sync.dma_start(dw_table[:].bitcast(I32), d_words[0].rearrange("p n t -> p (n t)").bitcast(I32))
+        n3_t = load_list(n3, "n3_t")
+        n1_t = load_list(n1, "n1_t")
+        n4_t = load_list(n4, "n4_t")
+        for q in range(4):
+            nc.gpsimd.dma_start(xs_table[32 * q : 32 * q + 4, :].bitcast(I32), x_scales[0, 4 * q : 4 * q + 4, :].bitcast(I32))
+
+        ds_picked = shared.tile([P, H], U8, name="ds_picked", offset=1792)
+        nc.vector.tensor_copy(ds_picked[:], ds_table[:].indirect(k1_t[:]))
+        ds_dealt = sb([P, H], U8, "ds_dealt")
+        nc.vector.tensor_copy(
+            ds_dealt[:].rearrange("p (t c) -> p t c", t=PACK), ds_picked[:].rearrange("p (c t) -> p t c", t=PACK))
+        ds_plane = ds_dealt
+        for j in range(1, 4):
+            nc.sync.dma_start(ds_plane[j:P:32, :].bitcast(I32), ds_dealt[8 * j : P : 32, :].bitcast(I32))
+        xw_table = shared.tile([P, T], U32, name="xw_table", offset=2048)
+        nc.sync.dma_start(xw_table[:].bitcast(I32), x_words[0].rearrange("p n t -> p (n t)").bitcast(I32))
+        dw_picked = shared.tile([P, H], U32, name="dw_picked", offset=0)
+        nc.vector.tensor_copy(dw_picked[:], dw_table[:].indirect(k1_t[:]))
+        dw_dealt = sb([P, H], U32, "dw_dealt")
+        nc.vector.tensor_copy(
+            dw_dealt[:].bitcast(I32).rearrange("p (t c) -> p t c", t=PACK),
+            dw_picked[:].bitcast(I32).rearrange("p (c t) -> p t c", t=PACK))
+        xs_picked = shared.tile([P, S], U8, name="xs_picked", offset=0, align_bytes=64)
+        nc.vector.tensor_copy(xs_picked[:], xs_table[:].indirect(offs_t[:]))
+        xw_picked = sb([P, S], U32, "xw_picked")
+        nc.vector.tensor_copy(xw_picked[:], xw_table[:].indirect(offs_t[:]))
+
+        gain = shared.tile([P, PACK], F32, name="gain", offset=20480)
+        nc.sync.dma_start(gain[:], gn.rearrange("(p t) o -> p (t o)", t=PACK))
+        ww_raw = shared.tile([P, 2 * N], U8, name="ww_raw", offset=20480 + 1024)
+        nc.sync.dma_start(ww_raw[:].bitcast(I32), w1_words[0].bitcast(I32))
+        ws_raw = shared.tile([P, N], U8, name="ws_raw", offset=20480 + 2048)
+        nc.gpsimd.memset(ws_raw[:].bitcast(I32), 0)
+        for q in range(4):
+            nc.sync.dma_start(ws_raw[32 * q : 32 * q + 4, :].bitcast(I32), w1_scales[0, 4 * q : 4 * q + 4, :].bitcast(I32))
+        mem_rows = mem.rearrange("(p t) u -> p t u", t=PACK)
+        out_rows = out_0.rearrange("(p t) u -> p t u", t=PACK)
+        page = [shared.tile([P, U], F32, name=f"page{t}", offset=4096 + 4 * U * t) for t in range(PACK)]
+        for t in range(PACK):
+            nc.sync.dma_start(page[t][:], mem_rows[:, t, :])
+
+        h = [sb([P, S], F32, f"h{t}") for t in range(PACK)]
+        for t in range(PACK):
+            acc = psum.tile([P, S], F32, name=f"hacc{t}")
+            cols = slice(t * P, (t + 1) * P)
+            nc.tensor.matmul_mx(
+                out=acc[:], lhsT=dw_dealt[:, cols].bitcast(FP8X4), lhsT_scale=ds_plane[:, cols],
+                rhs=xw_picked[:].bitcast(FP8X4), rhs_scale=xs_picked[:], start=True, stop=True)
+            nc.scalar.activation(h[t][:], acc[:], COPY, scale=0.0625)
+
+        ww = shared.tile([P, 2 * N], U8, name="ww", offset=2048, align_bytes=64)
+        nc.vector.tensor_copy(
+            ww[:].rearrange("p (t c b) -> p t c b", t=PACK, b=2), ww_raw[:].rearrange("p (c t b) -> p t c b", t=PACK, b=2))
+        ws = shared.tile([P, N], U8, name="ws", offset=3072, align_bytes=64)
+        nc.vector.tensor_copy(
+            ws[:].rearrange("p (t c) -> p t c", t=PACK), ws_raw[:].rearrange("p (c t) -> p t c", t=PACK))
+
+        h2 = [[None] * PACK for c in range(CHUNKS)]
+
+        def neighbour_step(c):
+            cols = slice(c * CHUNK, (c + 1) * CHUNK)
+            at2 = sb([P, PACK, CHUNK], F32, f"at2_{c}")
+            at3 = sb([P, PACK, CHUNK], F32, f"at3_{c}")
+            larger = sb([P, PACK, CHUNK], F32, f"larger{c}")
+            rest = sb([P, PACK, CHUNK], F32, f"rest{c}")
+            y = sb([P, PACK, CHUNK], F32, f"y{c}")
+            for t in range(PACK + 1):
+                if t < PACK:
+                    nc.scalar.activation(at2[:, t, :], h[t][:].indirect(entries(n2_t, c)), COPY)
+                    if c == 0 and t == 0:
+                        nc.vector.tensor_copy(at3[:, t, :], h[t][:].indirect(entries(n3_t, c)))
+                    else:
+                        nc.scalar.activation(at3[:, t, :], h[t][:].indirect(entries(n3_t, c)), COPY)
+                if t > 0:
+                    nc.vector.tensor_tensor(rest[:, t - 1, :], h[t - 1][:].indirect(entries(n1_t, c)), larger[:, t - 1, :], ALU.subtract)
+                if t < PACK:
+                    nc.vector.tensor_tensor(larger[:, t, :], at2[:, t, :], at3[:, t, :], ALU.max)
+                if t > 0:
+                    nc.vector.tensor_tensor(y[:, t - 1, :], rest[:, t - 1, :], h[t - 1][:, cols], ALU.add)
+            z = sb([P, CHUNK * PACK], BF16, f"z{c}")
+            nc.vector.tensor_tensor(
+                z[:].rearrange("p (c i t) -> p c t i", i=4, t=PACK),
+                y[:].rearrange("p t (c i) -> p c t i", i=4),
+                gain[:].unsqueeze(1).unsqueeze(3).to_broadcast([P, CHUNK // 4, PACK, 4]),
+                ALU.mult)
+            z_words = sb([P, CHUNK], U32, f"z_words{c}")
+            z_scales = sb([P, CHUNK], U8, f"z_scales{c}")
+            nc.vector.quantize_mx(out=z_words[:].bitcast(FP8X4), scales=z_scales[:], in_=z[:])
+            return z_words, z_scales
+
+        def second_product(c, z_words, z_scales, engine_copy):
+            for pair in range(PACK // 2):
+                acc = psum.tile([P, 2, CHUNK], F32, name=f"oacc{c}_{pair}")
+                for u in range(2):
+                    t = 2 * pair + u
+                    nc.tensor.matmul_mx(
+                        out=acc[:, u, :], lhsT=ww[:, 2 * t * P : 2 * (t + 1) * P].bitcast(FP4X4),
+                        lhsT_scale=ws[:, t * P : (t + 1) * P],
+                        rhs=z_words[:].bitcast(FP8X4), rhs_scale=z_scales[:], start=True, stop=True)
+                res = sb([P, 2, CHUNK], F32, f"h2_{c}_{pair}")
+                engine_copy(res[:], acc[:])
+                for u in range(2):
+                    h2[c][2 * pair + u] = res[:, u, :]
+
+        def scatter_scalar(c, t):
+            nc.scalar.activation(page[t][:].indirect(entries(n4_t, c)), h2[c][t], COPY)
+
+        def scatter_vector(c, t):
+            nc.vector.tensor_copy(page[t][:].indirect(entries(n4_t, c)), h2[c][t])
+
+        first = neighbour_step(0)
+        second_product(0, *first, nc.scalar.copy)
+        second = neighbour_step(1)
+        for t in range(PACK):
+            scatter_scalar(0, t)
+        second_product(1, *second, nc.vector.tensor_copy)
+
+        SPLIT = 576
+        parts = [(0, SPLIT), (SPLIT, U)]
+        planar = [sb([P, PACK, hi - lo], BF16, f"planar{lo}") for lo, hi in parts]
+        for t in range(PACK):
+            if t < 2:
+                scatter_vector(1, t)
+            else:
+                scatter_scalar(1, t)
+            nc.sync.dma_start(out_rows[:, t, :], page[t][:])
+        for t in range(PACK):
+            nc.vector.tensor_copy(planar[0][:, t, :], page[t][:, :SPLIT])
+            if t < PACK - 1:
+                nc.vector.tensor_copy(planar[1][:, t, :], page[t][:, SPLIT:])
+            else:
+                nc.scalar.copy(planar[1][:, t, :], page[t][:, SPLIT:])
+
+        o_scales = sb([P, U], U8, "o_scales")
+        nc.gpsimd.memset(o_scales[:].bitcast(I32), 0)
+        words_out = out_1[0].rearrange("p n t -> p (n t)").bitcast(I32)
+        PIECE = 256
+        woven = [sb([P, PIECE * PACK], BF16, f"woven{s}") for s in range(U // PIECE)]
+
+        def weave(copy, part, lo, hi):
+            s = lo // PIECE
+            base = parts[part][0]
+            dst = woven[s][:, (lo - s * PIECE) * PACK : (hi - s * PIECE) * PACK].rearrange("p (c i t) -> p c t i", i=4, t=PACK)
+            copy(dst, planar[part][:, :, lo - base : hi - base].rearrange("p t (c i) -> p c t i", i=4))
+
+        def quantise(s):
+            cols = slice(s * PIECE, (s + 1) * PIECE)
+            o_words = sb([P, PIECE], U32, f"o_words{s}")
+            nc.vector.quantize_mx(out=o_words[:].bitcast(FP8X4), scales=o_scales[:, cols], in_=woven[s][:])
+            nc.sync.dma_start(words_out[:, cols], o_words[:].bitcast(I32))
+
+        weave(nc.scalar.copy, 1, SPLIT, 3 * PIECE)
+        weave(nc.scalar.copy, 1, 3 * PIECE, U)
+        weave(nc.vector.tensor_copy, 0, 0, PIECE)
+        weave(nc.vector.tensor_copy, 0, PIECE, 2 * PIECE)
+        quantise(0)
+        weave(nc.vector.tensor_copy, 0, 2 * PIECE, SPLIT)
+        for s in range(1, U // PIECE):
+            quantise(s)
+        for q in range(4):
+            queue = nc.sync if q % 2 == 0 else nc.scalar
+            queue.dma_start(out_2[0, 4 * q : 4 * q + 4, :].bitcast(I32), o_scales[32 * q : 32 * q + 4, :].bitcast(I32))

@@ -45,72 +45,86 @@ def tile_picked_pqlaytrimpage_none_po_kernel(
         def sb(shape, dtype, name):
             return keep.tile(shape, dtype, name=name, align_bytes=64)
 
-        ds_table = sb([P, G], U8, "ds_table")
-        xs_table = shared.tile([P, T], U8, name="xs_table", offset=15360)
-        nc.gpsimd.memset(xs_table[:].bitcast(I32), 0)
+        def at(shape, dtype, name, offset):
+            return shared.tile(shape, dtype, name=name, offset=offset, align_bytes=64)
 
+        def load_scale_rows(tile, src):
+            nc.sync.dma_start(tile[0:P:8, :].bitcast(I32), src[0].bitcast(I32))
+
+        def move_scale_rows(plane):
+            for j in range(1, 4):
+                nc.sync.dma_start(plane[j:P:32, :].bitcast(I32), plane[8 * j : P : 32, :].bitcast(I32))
+
+        ds_table = sb([P, G], U8, "ds_table")
+        nc.vector.memset(ds_table[:].bitcast(I32), 0)
+        xs_table = sb([P, T], U8, "xs_table")
+        nc.vector.memset(xs_table[:].bitcast(I32), 0)
         k1_t = load_list(k1, "k1_t")
-        nc.sync.dma_start(ds_table[:].bitcast(I32), d_scales[0].bitcast(I32).unsqueeze(1).to_broadcast([16, 8, G // 4]))
         offs_t = load_list(offs, "offs_t")
         n2_t = load_list(n2, "n2_t")
-        dw_table = shared.tile([P, G], U32, name="dw_table", offset=20480)
-        nc.sync.dma_start(dw_table[:].bitcast(I32), d_words[0].rearrange("p n t -> p (n t)").bitcast(I32))
         n3_t = load_list(n3, "n3_t")
+        load_scale_rows(ds_table, d_scales)
         n1_t = load_list(n1, "n1_t")
-        n4_t = load_list(n4, "n4_t")
-        for q in range(4):
-            nc.gpsimd.dma_start(xs_table[32 * q : 32 * q + 4, :].bitcast(I32), x_scales[0, 4 * q : 4 * q + 4, :].bitcast(I32))
-
-        ds_picked = shared.tile([P, H], U8, name="ds_picked", offset=1792)
-        nc.vector.tensor_copy(ds_picked[:], ds_table[:].indirect(k1_t[:]))
-        ds_dealt = sb([P, H], U8, "ds_dealt")
-        nc.vector.tensor_copy(
-            ds_dealt[:].rearrange("p (t c) -> p t c", t=PACK), ds_picked[:].rearrange("p (c t) -> p t c", t=PACK))
-        ds_plane = ds_dealt
-        for j in range(1, 4):
-            nc.sync.dma_start(ds_plane[j:P:32, :].bitcast(I32), ds_dealt[8 * j : P : 32, :].bitcast(I32))
-        xw_table = shared.tile([P, T], U32, name="xw_table", offset=2048)
+        load_scale_rows(xs_table, x_scales)
+        dw_table = at([P, G], U32, "dw_table", 20480)
+        nc.sync.dma_start(dw_table[:].bitcast(I32), d_words[0].rearrange("p n t -> p (n t)").bitcast(I32))
+        xw_table = at([P, T], U32, "xw_table", 2048)
         nc.sync.dma_start(xw_table[:].bitcast(I32), x_words[0].rearrange("p n t -> p (n t)").bitcast(I32))
-        dw_picked = shared.tile([P, H], U32, name="dw_picked", offset=0)
-        nc.vector.tensor_copy(dw_picked[:], dw_table[:].indirect(k1_t[:]))
-        dw_dealt = sb([P, H], U32, "dw_dealt")
-        nc.vector.tensor_copy(
-            dw_dealt[:].bitcast(I32).rearrange("p (t c) -> p t c", t=PACK),
-            dw_picked[:].bitcast(I32).rearrange("p (c t) -> p t c", t=PACK))
-        xs_picked = shared.tile([P, S], U8, name="xs_picked", offset=0, align_bytes=64)
-        nc.vector.tensor_copy(xs_picked[:], xs_table[:].indirect(offs_t[:]))
-        xw_picked = sb([P, S], U32, "xw_picked")
-        nc.vector.tensor_copy(xw_picked[:], xw_table[:].indirect(offs_t[:]))
+        n4_t = load_list(n4, "n4_t")
 
-        gain = shared.tile([P, PACK], F32, name="gain", offset=20480)
-        nc.sync.dma_start(gain[:], gn.rearrange("(p t) o -> p (t o)", t=PACK))
-        ww_raw = shared.tile([P, 2 * N], U8, name="ww_raw", offset=20480 + 1024)
+        ds_picked = at([P, H], U8, "ds_picked", 0)
+        nc.vector.tensor_copy(ds_picked[:], ds_table[:].indirect(k1_t[:]))
+        xs_picked = at([P, S], U8, "xs_picked", 512)
+        nc.vector.tensor_copy(xs_picked[:], xs_table[:].indirect(offs_t[:]))
+        planes = sb([P, H + S], U8, "planes")
+        nc.vector.tensor_copy(
+            planes[:, :H].rearrange("p (t g i) -> p g t i", t=PACK, i=16), ds_picked[:].rearrange("p (g i t) -> p g t i", t=PACK, i=16))
+        nc.vector.tensor_copy(planes[:, H:].bitcast(I32), xs_picked[:].bitcast(I32))
+        move_scale_rows(planes)
+        dw_picked = sb([P, H], U32, "dw_picked")
+        nc.vector.tensor_copy(dw_picked[:], dw_table[:].indirect(k1_t[:]))
+        dw_dealt = at([P, H], U32, "dw_dealt", 16384)
+        xw_picked = at([P, S], U32, "xw_picked", 12288)
+        nc.vector.tensor_copy(xw_picked[:, :CHUNK], xw_table[:].indirect(entries(offs_t, 0)))
+        nc.vector.tensor_copy(
+            dw_dealt[:].bitcast(I32).rearrange("p (t g i) -> p g t i", t=PACK, i=4),
+            dw_picked[:].bitcast(I32).rearrange("p (g i t) -> p g t i", t=PACK, i=4))
+        nc.vector.tensor_copy(xw_picked[:, CHUNK:], xw_table[:].indirect(entries(offs_t, 1)))
+
+        ww_raw = at([P, 2 * N], U8, "ww_raw", 20480)
         nc.sync.dma_start(ww_raw[:].bitcast(I32), w1_words[0].bitcast(I32))
-        ws_raw = shared.tile([P, N], U8, name="ws_raw", offset=20480 + 2048)
+        ws_raw = at([P, N], U8, "ws_raw", 20480 + 1024)
         nc.gpsimd.memset(ws_raw[:].bitcast(I32), 0)
-        for q in range(4):
-            nc.sync.dma_start(ws_raw[32 * q : 32 * q + 4, :].bitcast(I32), w1_scales[0, 4 * q : 4 * q + 4, :].bitcast(I32))
+        load_scale_rows(ws_raw, w1_scales)
+        gain = at([P, PACK], F32, "gain", 20480 + 2048)
+        nc.sync.dma_start(gain[:], gn.rearrange("(p t) o -> p (t o)", t=PACK))
         mem_rows = mem.rearrange("(p t) u -> p t u", t=PACK)
         out_rows = out_0.rearrange("(p t) u -> p t u", t=PACK)
-        page = [shared.tile([P, U], F32, name=f"page{t}", offset=4096 + 4 * U * t) for t in range(PACK)]
+        page = [at([P, U], F32, f"page{t}", 4096 + 4 * U * t) for t in range(PACK)]
         for t in range(PACK):
             nc.sync.dma_start(page[t][:], mem_rows[:, t, :])
 
         h = [sb([P, S], F32, f"h{t}") for t in range(PACK)]
-        for t in range(PACK):
-            acc = psum.tile([P, S], F32, name=f"hacc{t}")
-            cols = slice(t * P, (t + 1) * P)
-            nc.tensor.matmul_mx(
-                out=acc[:], lhsT=dw_dealt[:, cols].bitcast(FP8X4), lhsT_scale=ds_plane[:, cols],
-                rhs=xw_picked[:].bitcast(FP8X4), rhs_scale=xs_picked[:], start=True, stop=True)
-            nc.scalar.activation(h[t][:], acc[:], COPY, scale=0.0625)
+        for c in range(CHUNKS):
+            tokens = slice(c * CHUNK, (c + 1) * CHUNK)
+            for pair in range(PACK // 2):
+                acc = psum.tile([P, 2, CHUNK], F32, name=f"hacc{c}_{pair}")
+                for u in range(2):
+                    cols = slice((2 * pair + u) * P, (2 * pair + u + 1) * P)
+                    nc.tensor.matmul_mx(
+                        out=acc[:, u, :], lhsT=dw_dealt[:, cols].bitcast(FP8X4), lhsT_scale=planes[:, cols],
+                        rhs=xw_picked[:, tokens].bitcast(FP8X4), rhs_scale=planes[:, H + c * CHUNK : H + (c + 1) * CHUNK],
+                        start=True, stop=True)
+                for u in range(2):
+                    nc.scalar.activation(h[2 * pair + u][:, tokens], acc[:, u, :], COPY, scale=0.0625)
 
         ww = shared.tile([P, 2 * N], U8, name="ww", offset=2048, align_bytes=64)
         nc.vector.tensor_copy(
-            ww[:].rearrange("p (t c b) -> p t c b", t=PACK, b=2), ww_raw[:].rearrange("p (c t b) -> p t c b", t=PACK, b=2))
+            ww[:].rearrange("p (t g i b) -> p g t i b", t=PACK, i=8, b=2), ww_raw[:].rearrange("p (g i t b) -> p g t i b", t=PACK, i=8, b=2))
         ws = shared.tile([P, N], U8, name="ws", offset=3072, align_bytes=64)
         nc.vector.tensor_copy(
-            ws[:].rearrange("p (t c) -> p t c", t=PACK), ws_raw[:].rearrange("p (c t) -> p t c", t=PACK))
+            ws[:].rearrange("p (t g i) -> p g t i", t=PACK, i=16), ws_raw[:].rearrange("p (g i t) -> p g t i", t=PACK, i=16))
+        move_scale_rows(ws)
 
         h2 = [[None] * PACK for c in range(CHUNKS)]
 
@@ -124,7 +138,7 @@ def tile_picked_pqlaytrimpage_none_po_kernel(
             for t in range(PACK + 1):
                 if t < PACK:
                     nc.scalar.activation(at2[:, t, :], h[t][:].indirect(entries(n2_t, c)), COPY)
-                    if c == 0 and t == 0:
+                    if c == 0 and t < 2:
                         nc.vector.tensor_copy(at3[:, t, :], h[t][:].indirect(entries(n3_t, c)))
                     else:
                         nc.scalar.activation(at3[:, t, :], h[t][:].indirect(entries(n3_t, c)), COPY)
@@ -173,20 +187,17 @@ def tile_picked_pqlaytrimpage_none_po_kernel(
         second_product(1, *second, nc.vector.tensor_copy)
 
         SPLIT = 576
-        parts = [(0, SPLIT), (SPLIT, U)]
-        planar = [sb([P, PACK, hi - lo], BF16, f"planar{lo}") for lo, hi in parts]
+        planar = sb([P, PACK, U], BF16, "planar")
         for t in range(PACK):
             if t < 2:
                 scatter_vector(1, t)
             else:
                 scatter_scalar(1, t)
             nc.sync.dma_start(out_rows[:, t, :], page[t][:])
-        for t in range(PACK):
-            nc.vector.tensor_copy(planar[0][:, t, :], page[t][:, :SPLIT])
-            if t < PACK - 1:
-                nc.vector.tensor_copy(planar[1][:, t, :], page[t][:, SPLIT:])
-            else:
-                nc.scalar.copy(planar[1][:, t, :], page[t][:, SPLIT:])
+        for t in range(PACK - 1):
+            nc.vector.tensor_copy(planar[:, t, :], page[t][:])
+        nc.vector.tensor_copy(planar[:, PACK - 1, :SPLIT], page[PACK - 1][:, :SPLIT])
+        nc.scalar.copy(planar[:, PACK - 1, SPLIT:], page[PACK - 1][:, SPLIT:])
 
         o_scales = sb([P, U], U8, "o_scales")
         nc.gpsimd.memset(o_scales[:].bitcast(I32), 0)
@@ -194,11 +205,10 @@ def tile_picked_pqlaytrimpage_none_po_kernel(
         PIECE = 256
         woven = [sb([P, PIECE * PACK], BF16, f"woven{s}") for s in range(U // PIECE)]
 
-        def weave(copy, part, lo, hi):
+        def weave(copy, lo, hi):
             s = lo // PIECE
-            base = parts[part][0]
             dst = woven[s][:, (lo - s * PIECE) * PACK : (hi - s * PIECE) * PACK].rearrange("p (c i t) -> p c t i", i=4, t=PACK)
-            copy(dst, planar[part][:, :, lo - base : hi - base].rearrange("p t (c i) -> p c t i", i=4))
+            copy(dst, planar[:, :, lo:hi].rearrange("p t (c i) -> p c t i", i=4))
 
         def quantise(s):
             cols = slice(s * PIECE, (s + 1) * PIECE)
@@ -206,12 +216,12 @@ def tile_picked_pqlaytrimpage_none_po_kernel(
             nc.vector.quantize_mx(out=o_words[:].bitcast(FP8X4), scales=o_scales[:, cols], in_=woven[s][:])
             nc.sync.dma_start(words_out[:, cols], o_words[:].bitcast(I32))
 
-        weave(nc.scalar.copy, 1, SPLIT, 3 * PIECE)
-        weave(nc.scalar.copy, 1, 3 * PIECE, U)
-        weave(nc.vector.tensor_copy, 0, 0, PIECE)
-        weave(nc.vector.tensor_copy, 0, PIECE, 2 * PIECE)
+        weave(nc.scalar.copy, SPLIT, 3 * PIECE)
+        weave(nc.scalar.copy, 3 * PIECE, U)
+        weave(nc.vector.tensor_copy, 0, PIECE)
+        weave(nc.vector.tensor_copy, PIECE, 2 * PIECE)
         quantise(0)
-        weave(nc.vector.tensor_copy, 0, 2 * PIECE, SPLIT)
+        weave(nc.vector.tensor_copy, 2 * PIECE, SPLIT)
         for s in range(1, U // PIECE):
             quantise(s)
         for q in range(4):

@@ -18,9 +18,26 @@ COPY = mybir.ActivationFunctionType.Copy
 
 P = 128
 PACK = 4
+LANES = 16
+BLOCK_PARTS = 8
+QUADRANT = 32
+H_SCALE = 0.0625
 CHUNK = 256
 CHUNKS = S // CHUNK
-LANES = 16
+VECTOR_FETCHES = 2
+VECTOR_SCATTERS = 2
+PIECE = 256
+SPLIT = 576
+
+PICKED_SCALES_AT = 0
+X_TABLE_AT = 2048
+W1_WORDS_AT = X_TABLE_AT
+W1_SCALES_AT = W1_WORDS_AT + 2 * N
+PAGE_AT = 4096
+PAGE_BYTES = 4 * U
+X_PICKED_AT = PAGE_AT + 2 * PAGE_BYTES
+D_DEALT_AT = PAGE_AT + 3 * PAGE_BYTES
+D_TABLE_AT = PAGE_AT + 4 * PAGE_BYTES
 
 
 def tile_picked_pqlaytrimpage_none_po_kernel(
@@ -39,8 +56,8 @@ def tile_picked_pqlaytrimpage_none_po_kernel(
             nc.sync.dma_start(tile[:], src)
             return tile
 
-        def entries(tile, c):
-            return tile[:, c * CHUNK // LANES : (c + 1) * CHUNK // LANES]
+        def entries(list_tile, c):
+            return list_tile[:, c * CHUNK // LANES : (c + 1) * CHUNK // LANES]
 
         def sb(shape, dtype, name):
             return keep.tile(shape, dtype, name=name, align_bytes=64)
@@ -49,11 +66,12 @@ def tile_picked_pqlaytrimpage_none_po_kernel(
             return shared.tile(shape, dtype, name=name, offset=offset, align_bytes=64)
 
         def load_scale_rows(tile, src):
-            nc.sync.dma_start(tile[0:P:8, :].bitcast(I32), src[0].bitcast(I32))
+            nc.sync.dma_start(tile[0:P:BLOCK_PARTS, :].bitcast(I32), src[0].bitcast(I32))
 
         def move_scale_rows(plane):
-            for j in range(1, 4):
-                nc.sync.dma_start(plane[j:P:32, :].bitcast(I32), plane[8 * j : P : 32, :].bitcast(I32))
+            for j in range(1, PACK):
+                nc.sync.dma_start(
+                    plane[j:P:QUADRANT, :].bitcast(I32), plane[BLOCK_PARTS * j : P : QUADRANT, :].bitcast(I32))
 
         ds_table = sb([P, G], U8, "ds_table")
         nc.vector.memset(ds_table[:].bitcast(I32), 0)
@@ -66,41 +84,43 @@ def tile_picked_pqlaytrimpage_none_po_kernel(
         load_scale_rows(ds_table, d_scales)
         n1_t = load_list(n1, "n1_t")
         load_scale_rows(xs_table, x_scales)
-        dw_table = at([P, G], U32, "dw_table", 20480)
+        dw_table = at([P, G], U32, "dw_table", D_TABLE_AT)
         nc.sync.dma_start(dw_table[:].bitcast(I32), d_words[0].rearrange("p n t -> p (n t)").bitcast(I32))
-        xw_table = at([P, T], U32, "xw_table", 2048)
+        xw_table = at([P, T], U32, "xw_table", X_TABLE_AT)
         nc.sync.dma_start(xw_table[:].bitcast(I32), x_words[0].rearrange("p n t -> p (n t)").bitcast(I32))
         n4_t = load_list(n4, "n4_t")
 
-        ds_picked = at([P, H], U8, "ds_picked", 0)
+        ds_picked = at([P, H], U8, "ds_picked", PICKED_SCALES_AT)
         nc.vector.tensor_copy(ds_picked[:], ds_table[:].indirect(k1_t[:]))
-        xs_picked = at([P, S], U8, "xs_picked", 512)
+        xs_picked = at([P, S], U8, "xs_picked", PICKED_SCALES_AT + H)
         nc.vector.tensor_copy(xs_picked[:], xs_table[:].indirect(offs_t[:]))
         planes = sb([P, H + S], U8, "planes")
         nc.vector.tensor_copy(
-            planes[:, :H].rearrange("p (t g i) -> p g t i", t=PACK, i=16), ds_picked[:].rearrange("p (g i t) -> p g t i", t=PACK, i=16))
+            planes[:, :H].rearrange("p (t g i) -> p g t i", t=PACK, i=16),
+            ds_picked[:].rearrange("p (g i t) -> p g t i", t=PACK, i=16))
         nc.vector.tensor_copy(planes[:, H:].bitcast(I32), xs_picked[:].bitcast(I32))
         move_scale_rows(planes)
+
         dw_picked = sb([P, H], U32, "dw_picked")
         nc.vector.tensor_copy(dw_picked[:], dw_table[:].indirect(k1_t[:]))
-        dw_dealt = at([P, H], U32, "dw_dealt", 16384)
-        xw_picked = at([P, S], U32, "xw_picked", 12288)
+        dw_dealt = at([P, H], U32, "dw_dealt", D_DEALT_AT)
+        xw_picked = at([P, S], U32, "xw_picked", X_PICKED_AT)
         nc.vector.tensor_copy(xw_picked[:, :CHUNK], xw_table[:].indirect(entries(offs_t, 0)))
         nc.vector.tensor_copy(
             dw_dealt[:].bitcast(I32).rearrange("p (t g i) -> p g t i", t=PACK, i=4),
             dw_picked[:].bitcast(I32).rearrange("p (g i t) -> p g t i", t=PACK, i=4))
         nc.vector.tensor_copy(xw_picked[:, CHUNK:], xw_table[:].indirect(entries(offs_t, 1)))
 
-        ww_raw = at([P, 2 * N], U8, "ww_raw", 20480)
+        ww_raw = at([P, 2 * N], U8, "ww_raw", D_TABLE_AT)
         nc.sync.dma_start(ww_raw[:].bitcast(I32), w1_words[0].bitcast(I32))
-        ws_raw = at([P, N], U8, "ws_raw", 20480 + 1024)
+        ws_raw = at([P, N], U8, "ws_raw", D_TABLE_AT + 2 * N)
         nc.gpsimd.memset(ws_raw[:].bitcast(I32), 0)
         load_scale_rows(ws_raw, w1_scales)
-        gain = at([P, PACK], F32, "gain", 20480 + 2048)
+        gain = at([P, PACK], F32, "gain", D_TABLE_AT + 4 * N)
         nc.sync.dma_start(gain[:], gn.rearrange("(p t) o -> p (t o)", t=PACK))
         mem_rows = mem.rearrange("(p t) u -> p t u", t=PACK)
         out_rows = out_0.rearrange("(p t) u -> p t u", t=PACK)
-        page = [at([P, U], F32, f"page{t}", 4096 + 4 * U * t) for t in range(PACK)]
+        page = [at([P, U], F32, f"page{t}", PAGE_AT + PAGE_BYTES * t) for t in range(PACK)]
         for t in range(PACK):
             nc.sync.dma_start(page[t][:], mem_rows[:, t, :])
 
@@ -113,23 +133,24 @@ def tile_picked_pqlaytrimpage_none_po_kernel(
                     cols = slice((2 * pair + u) * P, (2 * pair + u + 1) * P)
                     nc.tensor.matmul_mx(
                         out=acc[:, u, :], lhsT=dw_dealt[:, cols].bitcast(FP8X4), lhsT_scale=planes[:, cols],
-                        rhs=xw_picked[:, tokens].bitcast(FP8X4), rhs_scale=planes[:, H + c * CHUNK : H + (c + 1) * CHUNK],
+                        rhs=xw_picked[:, tokens].bitcast(FP8X4),
+                        rhs_scale=planes[:, H + c * CHUNK : H + (c + 1) * CHUNK],
                         start=True, stop=True)
                 for u in range(2):
-                    nc.scalar.activation(h[2 * pair + u][:, tokens], acc[:, u, :], COPY, scale=0.0625)
+                    nc.scalar.activation(h[2 * pair + u][:, tokens], acc[:, u, :], COPY, scale=H_SCALE)
 
-        ww = shared.tile([P, 2 * N], U8, name="ww", offset=2048, align_bytes=64)
+        ww = at([P, 2 * N], U8, "ww", W1_WORDS_AT)
         nc.vector.tensor_copy(
-            ww[:].rearrange("p (t g i b) -> p g t i b", t=PACK, i=8, b=2), ww_raw[:].rearrange("p (g i t b) -> p g t i b", t=PACK, i=8, b=2))
-        ws = shared.tile([P, N], U8, name="ws", offset=3072, align_bytes=64)
+            ww[:].rearrange("p (t g i b) -> p g t i b", t=PACK, i=8, b=2),
+            ww_raw[:].rearrange("p (g i t b) -> p g t i b", t=PACK, i=8, b=2))
+        ws = at([P, N], U8, "ws", W1_SCALES_AT)
         nc.vector.tensor_copy(
-            ws[:].rearrange("p (t g i) -> p g t i", t=PACK, i=16), ws_raw[:].rearrange("p (g i t) -> p g t i", t=PACK, i=16))
+            ws[:].rearrange("p (t g i) -> p g t i", t=PACK, i=16),
+            ws_raw[:].rearrange("p (g i t) -> p g t i", t=PACK, i=16))
         move_scale_rows(ws)
 
-        h2 = [[None] * PACK for c in range(CHUNKS)]
-
         def neighbour_step(c):
-            cols = slice(c * CHUNK, (c + 1) * CHUNK)
+            tokens = slice(c * CHUNK, (c + 1) * CHUNK)
             at2 = sb([P, PACK, CHUNK], F32, f"at2_{c}")
             at3 = sb([P, PACK, CHUNK], F32, f"at3_{c}")
             larger = sb([P, PACK, CHUNK], F32, f"larger{c}")
@@ -138,20 +159,21 @@ def tile_picked_pqlaytrimpage_none_po_kernel(
             for t in range(PACK + 1):
                 if t < PACK:
                     nc.scalar.activation(at2[:, t, :], h[t][:].indirect(entries(n2_t, c)), COPY)
-                    if c == 0 and t < 2:
+                    if c == 0 and t < VECTOR_FETCHES:
                         nc.vector.tensor_copy(at3[:, t, :], h[t][:].indirect(entries(n3_t, c)))
                     else:
                         nc.scalar.activation(at3[:, t, :], h[t][:].indirect(entries(n3_t, c)), COPY)
                 if t > 0:
-                    nc.vector.tensor_tensor(rest[:, t - 1, :], h[t - 1][:].indirect(entries(n1_t, c)), larger[:, t - 1, :], ALU.subtract)
+                    nc.vector.tensor_tensor(
+                        rest[:, t - 1, :], h[t - 1][:].indirect(entries(n1_t, c)), larger[:, t - 1, :], ALU.subtract)
                 if t < PACK:
                     nc.vector.tensor_tensor(larger[:, t, :], at2[:, t, :], at3[:, t, :], ALU.max)
                 if t > 0:
-                    nc.vector.tensor_tensor(y[:, t - 1, :], rest[:, t - 1, :], h[t - 1][:, cols], ALU.add)
+                    nc.vector.tensor_tensor(y[:, t - 1, :], rest[:, t - 1, :], h[t - 1][:, tokens], ALU.add)
             z = sb([P, CHUNK * PACK], BF16, f"z{c}")
             nc.vector.tensor_tensor(
-                z[:].rearrange("p (c i t) -> p c t i", i=4, t=PACK),
-                y[:].rearrange("p t (c i) -> p c t i", i=4),
+                z[:].rearrange("p (g i t) -> p g t i", i=4, t=PACK),
+                y[:].rearrange("p t (g i) -> p g t i", i=4),
                 gain[:].unsqueeze(1).unsqueeze(3).to_broadcast([P, CHUNK // 4, PACK, 4]),
                 ALU.mult)
             z_words = sb([P, CHUNK], U32, f"z_words{c}")
@@ -159,7 +181,8 @@ def tile_picked_pqlaytrimpage_none_po_kernel(
             nc.vector.quantize_mx(out=z_words[:].bitcast(FP8X4), scales=z_scales[:], in_=z[:])
             return z_words, z_scales
 
-        def second_product(c, z_words, z_scales, engine_copy):
+        def second_product(c, z_words, z_scales, copy_out):
+            tiles = []
             for pair in range(PACK // 2):
                 acc = psum.tile([P, 2, CHUNK], F32, name=f"oacc{c}_{pair}")
                 for u in range(2):
@@ -169,46 +192,42 @@ def tile_picked_pqlaytrimpage_none_po_kernel(
                         lhsT_scale=ws[:, t * P : (t + 1) * P],
                         rhs=z_words[:].bitcast(FP8X4), rhs_scale=z_scales[:], start=True, stop=True)
                 res = sb([P, 2, CHUNK], F32, f"h2_{c}_{pair}")
-                engine_copy(res[:], acc[:])
-                for u in range(2):
-                    h2[c][2 * pair + u] = res[:, u, :]
+                copy_out(res[:], acc[:])
+                tiles.extend([res[:, 0, :], res[:, 1, :]])
+            return tiles
 
-        def scatter_scalar(c, t):
-            nc.scalar.activation(page[t][:].indirect(entries(n4_t, c)), h2[c][t], COPY)
+        def scatter_on_scalar(c, t, values):
+            nc.scalar.activation(page[t][:].indirect(entries(n4_t, c)), values, COPY)
 
-        def scatter_vector(c, t):
-            nc.vector.tensor_copy(page[t][:].indirect(entries(n4_t, c)), h2[c][t])
+        def scatter_on_vector(c, t, values):
+            nc.vector.tensor_copy(page[t][:].indirect(entries(n4_t, c)), values)
 
-        first = neighbour_step(0)
-        second_product(0, *first, nc.scalar.copy)
-        second = neighbour_step(1)
+        h2_first = second_product(0, *neighbour_step(0), nc.scalar.copy)
+        z_second = neighbour_step(1)
         for t in range(PACK):
-            scatter_scalar(0, t)
-        second_product(1, *second, nc.vector.tensor_copy)
+            scatter_on_scalar(0, t, h2_first[t])
+        h2_second = second_product(1, *z_second, nc.vector.tensor_copy)
 
-        SPLIT = 576
-        planar = sb([P, PACK, U], BF16, "planar")
+        rounded = sb([P, PACK, U], BF16, "rounded")
         for t in range(PACK):
-            if t < 2:
-                scatter_vector(1, t)
-            else:
-                scatter_scalar(1, t)
+            scatter = scatter_on_vector if t < VECTOR_SCATTERS else scatter_on_scalar
+            scatter(1, t, h2_second[t])
             nc.sync.dma_start(out_rows[:, t, :], page[t][:])
-        for t in range(PACK - 1):
-            nc.vector.tensor_copy(planar[:, t, :], page[t][:])
-        nc.vector.tensor_copy(planar[:, PACK - 1, :SPLIT], page[PACK - 1][:, :SPLIT])
-        nc.scalar.copy(planar[:, PACK - 1, SPLIT:], page[PACK - 1][:, SPLIT:])
+        last = PACK - 1
+        for t in range(last):
+            nc.vector.tensor_copy(rounded[:, t, :], page[t][:])
+        nc.vector.tensor_copy(rounded[:, last, :SPLIT], page[last][:, :SPLIT])
+        nc.scalar.copy(rounded[:, last, SPLIT:], page[last][:, SPLIT:])
 
         o_scales = sb([P, U], U8, "o_scales")
-        nc.gpsimd.memset(o_scales[:].bitcast(I32), 0)
         words_out = out_1[0].rearrange("p n t -> p (n t)").bitcast(I32)
-        PIECE = 256
         woven = [sb([P, PIECE * PACK], BF16, f"woven{s}") for s in range(U // PIECE)]
 
         def weave(copy, lo, hi):
             s = lo // PIECE
-            dst = woven[s][:, (lo - s * PIECE) * PACK : (hi - s * PIECE) * PACK].rearrange("p (c i t) -> p c t i", i=4, t=PACK)
-            copy(dst, planar[:, :, lo:hi].rearrange("p t (c i) -> p c t i", i=4))
+            dst = woven[s][:, (lo - s * PIECE) * PACK : (hi - s * PIECE) * PACK]
+            copy(dst.rearrange("p (g i t) -> p g t i", i=4, t=PACK),
+                 rounded[:, :, lo:hi].rearrange("p t (g i) -> p g t i", i=4))
 
         def quantise(s):
             cols = slice(s * PIECE, (s + 1) * PIECE)
@@ -224,6 +243,8 @@ def tile_picked_pqlaytrimpage_none_po_kernel(
         weave(nc.vector.tensor_copy, 2 * PIECE, SPLIT)
         for s in range(1, U // PIECE):
             quantise(s)
-        for q in range(4):
+        for q in range(P // QUADRANT):
             queue = nc.sync if q % 2 == 0 else nc.scalar
-            queue.dma_start(out_2[0, 4 * q : 4 * q + 4, :].bitcast(I32), o_scales[32 * q : 32 * q + 4, :].bitcast(I32))
+            queue.dma_start(
+                out_2[0, PACK * q : PACK * (q + 1), :].bitcast(I32),
+                o_scales[QUADRANT * q : QUADRANT * q + PACK, :].bitcast(I32))

from contextlib import ExitStack

import concourse.mybir as mybir

K, T, S, N, G, H, U = 512, 2048, 512, 512, 2048, 512, 1024
FLOPS = 2 * K * H * S + 2 * H * N * S

F32 = mybir.dt.float32
BF16 = mybir.dt.bfloat16
I32 = mybir.dt.int32
U32 = mybir.dt.uint32
U16 = mybir.dt.uint16
U8 = mybir.dt.uint8
FP8X4 = mybir.dt.float8_e4m3fn_x4
FP4X4 = mybir.dt.float4_e2m1fn_x4
ALU = mybir.AluOpType
COPY = mybir.ActivationFunctionType.Copy

P = 128
PACK = 4
LANES = 16
BLOCK_PARTS = 8
QUADRANT = 32
H_SCALE = 0.0625
CHUNK = 256
CHUNKS = S // CHUNK
VECTOR_FETCHES = 2
VECTOR_SCATTERS = 2
PIECE = 256
SPLIT = 576

PICKED_SCALES_AT = 0
X_TABLE_AT = 2048
W1_WORDS_AT = X_TABLE_AT
W1_SCALES_AT = W1_WORDS_AT + 2 * N
PAGE_AT = 4096
PAGE_BYTES = 4 * U
X_PICKED_AT = PAGE_AT + 2 * PAGE_BYTES
D_DEALT_AT = PAGE_AT + 3 * PAGE_BYTES
D_TABLE_AT = PAGE_AT + 4 * PAGE_BYTES


def tile_picked_pqlaytrimpage_none_po_kernel(
    tc, x_words, x_scales, d_words, d_scales, gn, w1_words, w1_scales, mem,
    offs, k1, n1, n2, n3, n4, out_0, out_1, out_2,
):
    nc = tc.nc
    with ExitStack() as ctx:
        lists = ctx.enter_context(tc.tile_pool(name="lists", bufs=1))
        keep = ctx.enter_context(tc.tile_pool(name="keep", bufs=1))
        shared = ctx.enter_context(tc.tile_pool(name="shared", bufs=1))
        psum = ctx.enter_context(tc.psum_pool(name="psum", bufs=1))

        def load_list(src, name):
            tile = lists.tile([P, S // LANES], U16, name=name)
            nc.sync.dma_start(tile[:], src)
            return tile

        def entries(list_tile, c):
            return list_tile[:, c * CHUNK // LANES : (c + 1) * CHUNK // LANES]

        def sb(shape, dtype, name):
            return keep.tile(shape, dtype, name=name, align_bytes=64)

        def at(shape, dtype, name, offset):
            return shared.tile(shape, dtype, name=name, offset=offset, align_bytes=64)

        def load_scale_rows(tile, src):
            nc.sync.dma_start(tile[0:P:BLOCK_PARTS, :].bitcast(I32), src[0].bitcast(I32))

        def move_scale_rows(plane):
            for j in range(1, PACK):
                nc.sync.dma_start(
                    plane[j:P:QUADRANT, :].bitcast(I32), plane[BLOCK_PARTS * j : P : QUADRANT, :].bitcast(I32))

        ds_table = sb([P, G], U8, "ds_table")
        nc.vector.memset(ds_table[:].bitcast(I32), 0)
        xs_table = sb([P, T], U8, "xs_table")
        nc.vector.memset(xs_table[:].bitcast(I32), 0)
        k1_t = load_list(k1, "k1_t")
        offs_t = load_list(offs, "offs_t")
        n2_t = load_list(n2, "n2_t")
        n3_t = load_list(n3, "n3_t")
        load_scale_rows(ds_table, d_scales)
        n1_t = load_list(n1, "n1_t")
        load_scale_rows(xs_table, x_scales)
        dw_table = at([P, G], U32, "dw_table", D_TABLE_AT)
        nc.sync.dma_start(dw_table[:].bitcast(I32), d_words[0].rearrange("p n t -> p (n t)").bitcast(I32))
        xw_table = at([P, T], U32, "xw_table", X_TABLE_AT)
        nc.sync.dma_start(xw_table[:].bitcast(I32), x_words[0].rearrange("p n t -> p (n t)").bitcast(I32))
        n4_t = load_list(n4, "n4_t")

        ds_picked = at([P, H], U8, "ds_picked", PICKED_SCALES_AT)
        nc.vector.tensor_copy(ds_picked[:], ds_table[:].indirect(k1_t[:]))
        xs_picked = at([P, S], U8, "xs_picked", PICKED_SCALES_AT + H)
        nc.vector.tensor_copy(xs_picked[:], xs_table[:].indirect(offs_t[:]))
        planes = sb([P, H + S], U8, "planes")
        nc.vector.tensor_copy(
            planes[:, :H].rearrange("p (t g i) -> p g t i", t=PACK, i=16),
            ds_picked[:].rearrange("p (g i t) -> p g t i", t=PACK, i=16))
        nc.vector.tensor_copy(planes[:, H:].bitcast(I32), xs_picked[:].bitcast(I32))
        move_scale_rows(planes)

        dw_picked = sb([P, H], U32, "dw_picked")
        nc.vector.tensor_copy(dw_picked[:], dw_table[:].indirect(k1_t[:]))
        dw_dealt = at([P, H], U32, "dw_dealt", D_DEALT_AT)
        xw_picked = at([P, S], U32, "xw_picked", X_PICKED_AT)
        nc.vector.tensor_copy(xw_picked[:, :CHUNK], xw_table[:].indirect(entries(offs_t, 0)))
        nc.vector.tensor_copy(
            dw_dealt[:].bitcast(I32).rearrange("p (t g i) -> p g t i", t=PACK, i=4),
            dw_picked[:].bitcast(I32).rearrange("p (g i t) -> p g t i", t=PACK, i=4))
        nc.vector.tensor_copy(xw_picked[:, CHUNK:], xw_table[:].indirect(entries(offs_t, 1)))

        ww_raw = at([P, 2 * N], U8, "ww_raw", D_TABLE_AT)
        nc.sync.dma_start(ww_raw[:].bitcast(I32), w1_words[0].bitcast(I32))
        ws_raw = at([P, N], U8, "ws_raw", D_TABLE_AT + 2 * N)
        nc.gpsimd.memset(ws_raw[:].bitcast(I32), 0)
        load_scale_rows(ws_raw, w1_scales)
        gain = at([P, PACK], F32, "gain", D_TABLE_AT + 4 * N)
        nc.sync.dma_start(gain[:], gn.rearrange("(p t) o -> p (t o)", t=PACK))
        mem_rows = mem.rearrange("(p t) u -> p t u", t=PACK)
        out_rows = out_0.rearrange("(p t) u -> p t u", t=PACK)
        page = [at([P, U], F32, f"page{t}", PAGE_AT + PAGE_BYTES * t) for t in range(PACK)]
        for t in range(PACK):
            nc.sync.dma_start(page[t][:], mem_rows[:, t, :])

        h = [sb([P, S], F32, f"h{t}") for t in range(PACK)]
        for c in range(CHUNKS):
            tokens = slice(c * CHUNK, (c + 1) * CHUNK)
            for pair in range(PACK // 2):
                acc = psum.tile([P, 2, CHUNK], F32, name=f"hacc{c}_{pair}")
                for u in range(2):
                    cols = slice((2 * pair + u) * P, (2 * pair + u + 1) * P)
                    nc.tensor.matmul_mx(
                        out=acc[:, u, :], lhsT=dw_dealt[:, cols].bitcast(FP8X4), lhsT_scale=planes[:, cols],
                        rhs=xw_picked[:, tokens].bitcast(FP8X4),
                        rhs_scale=planes[:, H + c * CHUNK : H + (c + 1) * CHUNK],
                        start=True, stop=True)
                for u in range(2):
                    nc.scalar.activation(h[2 * pair + u][:, tokens], acc[:, u, :], COPY, scale=H_SCALE)

        ww = at([P, 2 * N], U8, "ww", W1_WORDS_AT)
        nc.vector.tensor_copy(
            ww[:].rearrange("p (t g i b) -> p g t i b", t=PACK, i=8, b=2),
            ww_raw[:].rearrange("p (g i t b) -> p g t i b", t=PACK, i=8, b=2))
        ws = at([P, N], U8, "ws", W1_SCALES_AT)
        nc.vector.tensor_copy(
            ws[:].rearrange("p (t g i) -> p g t i", t=PACK, i=16),
            ws_raw[:].rearrange("p (g i t) -> p g t i", t=PACK, i=16))
        move_scale_rows(ws)

        def neighbour_step(c):
            tokens = slice(c * CHUNK, (c + 1) * CHUNK)
            at2 = sb([P, PACK, CHUNK], F32, f"at2_{c}")
            at3 = sb([P, PACK, CHUNK], F32, f"at3_{c}")
            larger = sb([P, PACK, CHUNK], F32, f"larger{c}")
            rest = sb([P, PACK, CHUNK], F32, f"rest{c}")
            y = sb([P, PACK, CHUNK], F32, f"y{c}")
            for t in range(PACK + 1):
                if t < PACK:
                    nc.scalar.activation(at2[:, t, :], h[t][:].indirect(entries(n2_t, c)), COPY)
                    if c == 0 and t < VECTOR_FETCHES:
                        nc.vector.tensor_copy(at3[:, t, :], h[t][:].indirect(entries(n3_t, c)))
                    else:
                        nc.scalar.activation(at3[:, t, :], h[t][:].indirect(entries(n3_t, c)), COPY)
                if t > 0:
                    nc.vector.tensor_tensor(
                        rest[:, t - 1, :], h[t - 1][:].indirect(entries(n1_t, c)), larger[:, t - 1, :], ALU.subtract)
                if t < PACK:
                    nc.vector.tensor_tensor(larger[:, t, :], at2[:, t, :], at3[:, t, :], ALU.max)
                if t > 0:
                    nc.vector.tensor_tensor(y[:, t - 1, :], rest[:, t - 1, :], h[t - 1][:, tokens], ALU.add)
            z = sb([P, CHUNK * PACK], BF16, f"z{c}")
            nc.vector.tensor_tensor(
                z[:].rearrange("p (g i t) -> p g t i", i=4, t=PACK),
                y[:].rearrange("p t (g i) -> p g t i", i=4),
                gain[:].unsqueeze(1).unsqueeze(3).to_broadcast([P, CHUNK // 4, PACK, 4]),
                ALU.mult)
            z_words = sb([P, CHUNK], U32, f"z_words{c}")
            z_scales = sb([P, CHUNK], U8, f"z_scales{c}")
            nc.vector.quantize_mx(out=z_words[:].bitcast(FP8X4), scales=z_scales[:], in_=z[:])
            return z_words, z_scales

        def second_product(c, z_words, z_scales, copy_out):
            tiles = []
            for pair in range(PACK // 2):
                acc = psum.tile([P, 2, CHUNK], F32, name=f"oacc{c}_{pair}")
                for u in range(2):
                    t = 2 * pair + u
                    nc.tensor.matmul_mx(
                        out=acc[:, u, :], lhsT=ww[:, 2 * t * P : 2 * (t + 1) * P].bitcast(FP4X4),
                        lhsT_scale=ws[:, t * P : (t + 1) * P],
                        rhs=z_words[:].bitcast(FP8X4), rhs_scale=z_scales[:], start=True, stop=True)
                res = sb([P, 2, CHUNK], F32, f"h2_{c}_{pair}")
                copy_out(res[:], acc[:])
                tiles.extend([res[:, 0, :], res[:, 1, :]])
            return tiles

        def scatter_on_scalar(c, t, values):
            nc.scalar.activation(page[t][:].indirect(entries(n4_t, c)), values, COPY)

        def scatter_on_vector(c, t, values):
            nc.vector.tensor_copy(page[t][:].indirect(entries(n4_t, c)), values)

        h2_first = second_product(0, *neighbour_step(0), nc.scalar.copy)
        z_second = neighbour_step(1)
        for t in range(PACK):
            scatter_on_scalar(0, t, h2_first[t])
        h2_second = second_product(1, *z_second, nc.vector.tensor_copy)

        rounded = sb([P, PACK, U], BF16, "rounded")
        for t in range(PACK):
            scatter = scatter_on_vector if t < VECTOR_SCATTERS else scatter_on_scalar
            scatter(1, t, h2_second[t])
            nc.sync.dma_start(out_rows[:, t, :], page[t][:])
        last = PACK - 1
        for t in range(last):
            nc.vector.tensor_copy(rounded[:, t, :], page[t][:])
        nc.vector.tensor_copy(rounded[:, last, :SPLIT], page[last][:, :SPLIT])
        nc.scalar.copy(rounded[:, last, SPLIT:], page[last][:, SPLIT:])

        o_scales = sb([P, U], U8, "o_scales")
        words_out = out_1[0].rearrange("p n t -> p (n t)").bitcast(I32)
        woven = [sb([P, PIECE * PACK], BF16, f"woven{s}") for s in range(U // PIECE)]

        def weave(copy, lo, hi):
            s = lo // PIECE
            dst = woven[s][:, (lo - s * PIECE) * PACK : (hi - s * PIECE) * PACK]
            copy(dst.rearrange("p (g i t) -> p g t i", i=4, t=PACK),
                 rounded[:, :, lo:hi].rearrange("p t (g i) -> p g t i", i=4))

        def quantise(s):
            cols = slice(s * PIECE, (s + 1) * PIECE)
            o_words = sb([P, PIECE], U32, f"o_words{s}")
            nc.vector.quantize_mx(out=o_words[:].bitcast(FP8X4), scales=o_scales[:, cols], in_=woven[s][:])
            nc.sync.dma_start(words_out[:, cols], o_words[:].bitcast(I32))

        weave(nc.scalar.copy, SPLIT, 3 * PIECE)
        weave(nc.scalar.copy, 3 * PIECE, U)
        weave(nc.vector.tensor_copy, 0, PIECE)
        weave(nc.vector.tensor_copy, PIECE, 2 * PIECE)
        quantise(0)
        weave(nc.vector.tensor_copy, 2 * PIECE, SPLIT)
        for s in range(1, U // PIECE):
            quantise(s)
        for q in range(P // QUADRANT):
            queue = nc.sync if q % 2 == 0 else nc.scalar
            queue.dma_start(
                out_2[0, PACK * q : PACK * (q + 1), :].bitcast(I32),
                o_scales[QUADRANT * q : QUADRANT * q + PACK, :].bitcast(I32))
